import numpy as np
import ml_dtypes


def mxq(x, axis, fmt="e4m3"):
    dtype, down = {"e4m3": (ml_dtypes.float8_e4m3fn, 7), "e5m2": (ml_dtypes.float8_e5m2, 14)}[fmt]
    v = np.moveaxis(np.asarray(x, np.float32).astype(ml_dtypes.bfloat16).astype(np.float64), axis, -1)
    blocks = v.reshape(v.shape[:-1] + (-1, 32))
    amax = np.abs(blocks).max(-1, keepdims=True)
    byte = np.maximum(np.where(amax > 0, np.frexp(amax)[1] - 1 + 127, 0) - down, 1)
    scale = np.exp2(byte - 127.0)
    codes = (blocks / scale).astype(np.float32).astype(dtype).astype(np.float64)
    return np.moveaxis((codes * scale).reshape(v.shape), -1, axis)


WIDE = False


def mx_kscale(k):
    if not WIDE:
        return np.ones(k)
    levels = np.array([10, -10, 5, -5, 0])
    if k % 512:
        return np.exp2(np.random.permutation(np.resize(levels, k // 32))).repeat(32)
    a = np.empty((k // 512, 16))
    for p in range(k // 512):
        a[p, :8] = np.random.permutation(np.resize(levels, 8))
        for g in range(8):
            far = levels[np.abs(levels - a[p, g]) >= 10]
            a[p, g + 8] = far[np.random.randint(len(far))]
    return np.exp2(a.ravel()).repeat(32)


def f64(x):
    return np.asarray(x).astype(np.float64)


def striped(idx):
    return np.tile(np.asarray(idx).reshape(-1, 16).T, (8, 1)).astype(np.uint16)


def unstriped(offs):
    return offs[:16].T.reshape(-1).astype(np.int64)


E2M1 = np.array([0.0, 0.5, 1.0, 1.5, 2.0, 3.0, 4.0, 6.0, -0.0, -0.5, -1.0, -1.5, -2.0, -3.0, -4.0, -6.0])


def pack_weight(w, fmt):
    k, n = w.shape
    w = f64(np.asarray(w, np.float32).astype(ml_dtypes.bfloat16)).reshape(k // 32, 32, n)
    amax = np.abs(w).max(1)
    if fmt == "e4m3":
        byte = np.frexp(amax)[1] - 1 + 127 - 7
    else:
        mant, ex = np.frexp(amax / 6.0)
        byte = np.where(mant > 0.5, ex, ex - 1) + 127
    byte = np.clip(np.where(amax > 0, byte, 1), 1, 254)
    scaled = (w * np.exp2(127.0 - byte)[:, None, :]).reshape(k, n).astype(np.float32)
    by_word = np.ascontiguousarray(scaled.reshape(k // 512, 128, 4, n).transpose(0, 1, 3, 2))
    if fmt == "e4m3":
        words = by_word.astype(ml_dtypes.float8_e4m3fn).view(np.uint8)
    else:
        c = by_word.astype(ml_dtypes.float4_e2m1fn).view(np.uint8) & 0xF
        words = (c[..., 0::2] | (c[..., 1::2] << 4)).reshape(k // 512, 128, 2 * n)
    return np.ascontiguousarray(words), np.ascontiguousarray(byte.astype(np.uint8).reshape(k // 512, 16, n))


def unpack_weight(words, scales, fmt):
    g, _, n = scales.shape
    words = np.ascontiguousarray(words).reshape(g, 128, n, -1)
    if fmt == "e4m3":
        vals = words.view(ml_dtypes.float8_e4m3fn).astype(np.float64)
    else:
        nib = np.empty((g, 128, n, 4), np.uint8)
        nib[..., 0::2] = words & 0xF
        nib[..., 1::2] = words >> 4
        vals = E2M1[nib]
    vals = vals * np.repeat(np.exp2(scales.astype(np.float64) - 127.0), 8, axis=1)[..., None]
    return vals.transpose(0, 1, 3, 2).reshape(g * 512, n)


B, N, T, D, DV, NQ = 2, 512, 2048, 512, 128, 256
PAGE = 64


def setup_inputs():
    n = np.random.standard_normal
    pages = np.random.permutation(T // PAGE)[:B * N // PAGE]
    idx = (pages[:, None] * PAGE + np.arange(PAGE)[None, :]).reshape(-1)
    s = mx_kscale(D)[:, None]
    u = np.ones(T)
    u[idx] = mx_kscale(B * N)
    r = np.random.uniform(0.5, 2.0, T)
    k = n((D, T)) / s
    v = n((DV, T)) / (u * r)
    kp = pack_weight(k, "e4m3")
    return {
        "qT": (n((B, D, NQ)) * s * (0.80 / np.sqrt(D))).astype(np.float32),
        "k_words": kp[0],
        "k_scales": kp[1],
        "vT": v.astype(np.float32),
        "vs": np.tile(u * r, (128, 1)).astype(np.float32),
        "offs": striped(idx),
    }


def reference(qT, k_words, k_scales, vT, vs, offs):
    idx = unstriped(offs)
    k = unpack_weight(k_words, k_scales, "e4m3")
    v = f64(vT)
    pick = lambda x: x[:, idx].reshape(x.shape[0], B, N).transpose(1, 0, 2)
    q = f64(qT)
    score = mxq(q, 1, "e4m3").transpose(0, 2, 1) @ pick(k)
    p = 1.0 / (1.0 + np.exp(-score))
    w = p * pick(f64(vs))[:, :1, :]
    y = mxq(w, 2, "e4m3") @ mxq(pick(v).transpose(0, 2, 1), 1, "e4m3")
    y = y / 16.0
    return y

@@ -1,0 +1,178 @@
+from contextlib import ExitStack
+
+import concourse.mybir as mybir
+from concourse.masks import make_identity
+
+B, N, T, D, DV, NQ = 2, 512, 2048, 512, 128, 256
+FLOPS = 2 * B * NQ * N * (D + DV)
+
+F32 = mybir.dt.float32
+BF16 = mybir.dt.bfloat16
+I32 = mybir.dt.int32
+U32 = mybir.dt.uint32
+U16 = mybir.dt.uint16
+U8 = mybir.dt.uint8
+FP8X4 = mybir.dt.float8_e4m3fn_x4
+ACT = mybir.ActivationFunctionType
+MULT = mybir.AluOpType.mult
+
+P = 128
+PACK = 4
+RUN = 8
+HALVES = NQ // P
+LIST_COLS = N // 16
+VS_ROW = P - 1
+
+
+def tile_attend_sigm_pgb2q256n512t2048_kernel(tc, qT, k_words, k_scales, vT, vs, offs, out):
+    nc = tc.nc
+    with ExitStack() as ctx:
+        keep = ctx.enter_context(tc.tile_pool(name="keep", bufs=1))
+        psum = ctx.enter_context(tc.psum_pool(name="psum", bufs=1))
+
+        offsets = keep.tile([P, B * LIST_COLS], U16, name="offsets")
+        nc.sync.dma_start(offsets[:], offs)
+
+        vs_pool = keep.tile([P, T], F32, name="vs_pool")
+        nc.vector.memset(vs_pool[0:VS_ROW, :], 0.0)
+        nc.sync.dma_start(vs_pool[VS_ROW:P, :], vs[0:1, :])
+
+        ks_pool = keep.tile([P, T], U8, name="ks_pool")
+        for quad in range(4):
+            rows = k_scales[0, 4 * quad : 4 * quad + 4, :].bitcast(I32)
+            nc.sync.dma_start(
+                ks_pool[32 * quad : 32 * quad + 32, :].bitcast(I32),
+                rows.unsqueeze(0).broadcast_to([8, 4, T // 4]),
+            )
+
+        q_raw = [keep.tile([P, PACK, NQ], F32, name="q_raw%d" % b) for b in range(B)]
+        kw_pool = keep.tile([P, T], U32, name="kw_pool")
+        v_pool = keep.tile([P, T], F32, name="v_pool", tag="values_then_weights", align_bytes=64)
+        nc.sync.dma_start(q_raw[0][:], qT[0].rearrange("(p j) q -> p j q", j=PACK))
+        nc.sync.dma_start(kw_pool[:].bitcast(I32), k_words[0].rearrange("p t r -> p (t r)").bitcast(I32))
+        nc.sync.dma_start(q_raw[1][:], qT[1].rearrange("(p j) q -> p j q", j=PACK))
+        nc.sync.dma_start(v_pool[:], vT)
+
+        ident_f32 = keep.tile([P, P], F32, name="ident_f32")
+        make_identity(nc, ident_f32[:])
+        ident_bf16 = keep.tile([P, P], BF16, name="ident_bf16")
+        make_identity(nc, ident_bf16[:])
+
+        def dealt(ap):
+            return ap.rearrange("p r (g i) -> p g r i", i=RUN)
+
+        def seq_list(b):
+            return offsets[:, b * LIST_COLS : (b + 1) * LIST_COLS]
+
+        vs_dealt = [keep.tile([P, PACK, P], F32, name="vs_dealt%d" % b) for b in range(B)]
+        for b in range(B):
+            nc.vector.tensor_copy(dealt(vs_dealt[b][:].bitcast(U32)), vs_pool[:].bitcast(U32).indirect(seq_list(b)))
+        ks_slots = keep.tile([P, B * N], U8, name="ks_slots")
+        nc.vector.tensor_copy(ks_slots[:], ks_pool[:].indirect(offsets[:]))
+        k_scale = keep.tile([P, B * N], U8, name="k_scale", align_bytes=64)
+        nc.vector.tensor_copy(
+            k_scale[:].bitcast(I32).rearrange("p (b r g w) -> p b r g w", b=B, r=PACK, w=RUN // 4),
+            ks_slots[:].bitcast(I32).rearrange("p (b g r w) -> p b r g w", b=B, r=PACK, w=RUN // 4),
+        )
+
+        q_bf16 = [keep.tile([P, NQ, PACK], BF16, name="q_bf16%d" % b, align_bytes=64) for b in range(B)]
+        nc.scalar.copy(q_bf16[0][:], q_raw[0][:].rearrange("p j q -> p q j"))
+
+        slot_scale = []
+        for b in range(B):
+            vs_turned = psum.tile([P, PACK, P], F32, name="vs_turned%d" % b)
+            for r in range(PACK):
+                nc.tensor.transpose(vs_turned[:, r, :], vs_dealt[b][:, r, :], ident_f32[:])
+            scale_b = keep.tile([P, PACK], F32, name="slot_scale%d" % b)
+            nc.scalar.copy(scale_b[:], vs_turned[:, :, VS_ROW])
+            slot_scale.append(scale_b)
+
+        nc.scalar.copy(q_bf16[1][:], q_raw[1][:].rearrange("p j q -> p q j"))
+
+        probs = {}
+        for b in range(B):
+            k_code = keep.tile([P, PACK, P], U32, name="k_code%d" % b, align_bytes=64)
+            nc.vector.tensor_copy(dealt(k_code[:]), kw_pool[:].indirect(seq_list(b)))
+            q_code = keep.tile([P, NQ], U32, name="q_code%d" % b, align_bytes=64)
+            q_scale = keep.tile([P, NQ], U8, name="q_scale%d" % b, align_bytes=64)
+            nc.vector.quantize_mx(
+                out=q_code[:].bitcast(FP8X4), scales=q_scale[:], in_=q_bf16[b][:].rearrange("p q j -> p (q j)")
+            )
+            for h in range(HALVES):
+                cols = slice(h * P, (h + 1) * P)
+                score = psum.tile([P, PACK, P], F32, name="score", tag="bank%d%d" % (b, h))
+                for r in range(PACK):
+                    nc.tensor.matmul_mx(
+                        out=score[:, r, :],
+                        lhsT=k_code[:, r, :].bitcast(FP8X4),
+                        lhsT_scale=k_scale[:, b * N + r * P : b * N + (r + 1) * P],
+                        rhs=q_code[:, cols].bitcast(FP8X4),
+                        rhs_scale=q_scale[:, cols],
+                        start=True,
+                        stop=True,
+                    )
+                prob = keep.tile([P, P, PACK], F32, name="prob%d%d" % (b, h))
+                nc.scalar.activation(prob[:], score[:].rearrange("p r q -> p q r"), ACT.Sigmoid)
+                probs[b, h] = prob
+
+        v_bf16 = []
+        for b in range(B):
+            v_slots = keep.tile([P, PACK, P], BF16, name="v_slots%d" % b)
+            nc.vector.tensor_copy(dealt(v_slots[:]), v_pool[:].indirect(seq_list(b)))
+            v_turned = psum.tile([P, PACK, DV], BF16, name="v_turned%d" % b)
+            for r in range(PACK):
+                nc.tensor.transpose(v_turned[:, r, :], v_slots[:, r, :], ident_bf16[:])
+            v_b = keep.tile([P, DV, PACK], BF16, name="v_bf16%d" % b, align_bytes=64)
+            nc.scalar.copy(v_b[:], v_turned[:].rearrange("p r e -> p e r"))
+            v_bf16.append(v_b)
+
+        w_bf16 = keep.tile([P, B * HALVES * P * PACK], BF16, name="w_bf16", tag="values_then_weights", align_bytes=64)
+        units = [(b, h) for b in range(B) for h in range(HALVES)]
+        v_mx = {}
+
+        def weights(u):
+            return w_bf16[:, u * P * PACK : (u + 1) * P * PACK]
+
+        def weigh(u):
+            b, h = units[u]
+            nc.vector.tensor_tensor(
+                weights(u).rearrange("p (q r) -> p q r", r=PACK),
+                probs[b, h][:],
+                slot_scale[b][:].unsqueeze(1).broadcast_to([P, P, PACK]),
+                MULT,
+            )
+
+        def quantize_values(b):
+            v_code = keep.tile([P, DV], U32, name="v_code%d" % b, align_bytes=64)
+            v_scale = keep.tile([P, DV], U8, name="v_scale%d" % b, align_bytes=64)
+            nc.vector.quantize_mx(
+                out=v_code[:].bitcast(FP8X4), scales=v_scale[:], in_=v_bf16[b][:].rearrange("p e r -> p (e r)")
+            )
+            v_mx[b] = (v_code, v_scale)
+
+        def finish(u):
+            b, h = units[u]
+            w_code = keep.tile([P, P], U32, name="w_code%d" % u, align_bytes=64)
+            w_scale = keep.tile([P, P], U8, name="w_scale%d" % u, align_bytes=64)
+            nc.vector.quantize_mx(out=w_code[:].bitcast(FP8X4), scales=w_scale[:], in_=weights(u))
+            y = psum.tile([P, DV], F32, name="y", tag="bank%d%d" % (b, h))
+            nc.tensor.matmul_mx(
+                out=y[:],
+                lhsT=w_code[:].bitcast(FP8X4),
+                lhsT_scale=w_scale[:],
+                rhs=v_mx[b][0][:].bitcast(FP8X4),
+                rhs_scale=v_mx[b][1][:],
+                start=True,
+                stop=True,
+            )
+            result = keep.tile([P, DV], F32, name="result%d" % u)
+            nc.scalar.activation(result[:], y[:], ACT.Copy, scale=1.0 / 16.0)
+            nc.sync.dma_start(out[b, h * P : (h + 1) * P, :], result[:])
+
+        weigh(0)
+        for u in range(1, len(units)):
+            weigh(u)
+            if units[u - 1][1] == 0:
+                quantize_values(units[u - 1][0])
+            finish(u - 1)
+        finish(len(units) - 1)

@@ -33,8 +33,13 @@ def tile_attend_sigm_pgb2q256n512t2048_kernel(tc, qT, k_words, k_scales, vT, vs,
         offsets = keep.tile([P, B * LIST_COLS], U16, name="offsets")
         nc.sync.dma_start(offsets[:], offs)
 
+        warm = keep.tile([P, 2], F32, name="warm")
+        nc.vector.memset(warm[:, 0:1], 0.0)
+        nc.scalar.activation(warm[:, 1:2], warm[:, 0:1], ACT.Sigmoid)
+
         vs_pool = keep.tile([P, T], F32, name="vs_pool")
-        nc.vector.memset(vs_pool[0:VS_ROW, :], 0.0)
+        nc.vector.memset(vs_pool[0:VS_ROW, 0 : T // 2], 0.0)
+        nc.gpsimd.memset(vs_pool[0:VS_ROW, T // 2 : T], 0.0)
         nc.sync.dma_start(vs_pool[VS_ROW:P, :], vs[0:1, :])
 
         ks_pool = keep.tile([P, T], U8, name="ks_pool")
@@ -45,13 +50,14 @@ def tile_attend_sigm_pgb2q256n512t2048_kernel(tc, qT, k_words, k_scales, vT, vs,
                 rows.unsqueeze(0).broadcast_to([8, 4, T // 4]),
             )
 
-        q_raw = [keep.tile([P, PACK, NQ], F32, name="q_raw%d" % b) for b in range(B)]
+        q_raw = [keep.tile([P, PACK, NQ], F32, name="q_raw", tag="stage%d" % b, align_bytes=64) for b in range(B)]
         kw_pool = keep.tile([P, T], U32, name="kw_pool")
-        v_pool = keep.tile([P, T], F32, name="v_pool", tag="values_then_weights", align_bytes=64)
-        nc.sync.dma_start(q_raw[0][:], qT[0].rearrange("(p j) q -> p j q", j=PACK))
+        v_raw = [keep.tile([P, T // 2], F32, name="v_raw%d" % c) for c in range(2)]
+        for c in range(2):
+            nc.sync.dma_start(v_raw[c][:], vT[:, c * (T // 2) : (c + 1) * (T // 2)])
         nc.sync.dma_start(kw_pool[:].bitcast(I32), k_words[0].rearrange("p t r -> p (t r)").bitcast(I32))
-        nc.sync.dma_start(q_raw[1][:], qT[1].rearrange("(p j) q -> p j q", j=PACK))
-        nc.sync.dma_start(v_pool[:], vT)
+        for b in range(B):
+            nc.sync.dma_start(q_raw[b][:], qT[b].rearrange("(p j) q -> p j q", j=PACK))
 
         ident_f32 = keep.tile([P, P], F32, name="ident_f32")
         make_identity(nc, ident_f32[:])
@@ -75,28 +81,39 @@ def tile_attend_sigm_pgb2q256n512t2048_kernel(tc, qT, k_words, k_scales, vT, vs,
             ks_slots[:].bitcast(I32).rearrange("p (b g r w) -> p b r g w", b=B, r=PACK, w=RUN // 4),
         )
 
-        q_bf16 = [keep.tile([P, NQ, PACK], BF16, name="q_bf16%d" % b, align_bytes=64) for b in range(B)]
-        nc.scalar.copy(q_bf16[0][:], q_raw[0][:].rearrange("p j q -> p q j"))
-
         slot_scale = []
         for b in range(B):
             vs_turned = psum.tile([P, PACK, P], F32, name="vs_turned%d" % b)
             for r in range(PACK):
                 nc.tensor.transpose(vs_turned[:, r, :], vs_dealt[b][:, r, :], ident_f32[:])
-            scale_b = keep.tile([P, PACK], F32, name="slot_scale%d" % b)
-            nc.scalar.copy(scale_b[:], vs_turned[:, :, VS_ROW])
-            slot_scale.append(scale_b)
+            slot_scale.append(vs_turned[:, :, VS_ROW])
 
-        nc.scalar.copy(q_bf16[1][:], q_raw[1][:].rearrange("p j q -> p q j"))
+        v_pool = keep.tile([P, T], BF16, name="v_pool")
+        for c in range(2):
+            nc.scalar.activation(v_pool[:, c * (T // 2) : (c + 1) * (T // 2)], v_raw[c][:], ACT.Copy)
+        v_bf16 = []
+        for b in range(B):
+            v_slots = keep.tile([P, PACK, P], BF16, name="v_slots%d" % b)
+            nc.scalar.activation(dealt(v_slots[:]), v_pool[:].indirect(seq_list(b)), ACT.Copy)
+            v_turned = psum.tile([P, PACK, DV], BF16, name="v_turned%d" % b)
+            for r in range(PACK):
+                nc.tensor.transpose(v_turned[:, r, :], v_slots[:, r, :], ident_bf16[:])
+            v_b = keep.tile([P, DV, PACK], BF16, name="v_bf16%d" % b, align_bytes=64)
+            nc.scalar.copy(v_b[:], v_turned[:].rearrange("p r e -> p e r"))
+            v_bf16.append(v_b)
 
         probs = {}
         for b in range(B):
-            k_code = keep.tile([P, PACK, P], U32, name="k_code%d" % b, align_bytes=64)
+            k_code = keep.tile([P, PACK, P], U32, name="k_code", tag="stage0" if b else "keys0", align_bytes=64)
             nc.vector.tensor_copy(dealt(k_code[:]), kw_pool[:].indirect(seq_list(b)))
+            q_bf16 = keep.tile([P, NQ, PACK], BF16, name="q_bf16", tag="queries_then_values%d" % b, align_bytes=64)
+            nc.vector.tensor_copy(
+                q_bf16[:].rearrange("p (c i) j -> p c j i", i=4), q_raw[b][:].rearrange("p j (c i) -> p c j i", i=4)
+            )
             q_code = keep.tile([P, NQ], U32, name="q_code%d" % b, align_bytes=64)
             q_scale = keep.tile([P, NQ], U8, name="q_scale%d" % b, align_bytes=64)
             nc.vector.quantize_mx(
-                out=q_code[:].bitcast(FP8X4), scales=q_scale[:], in_=q_bf16[b][:].rearrange("p q j -> p (q j)")
+                out=q_code[:].bitcast(FP8X4), scales=q_scale[:], in_=q_bf16[:].rearrange("p q j -> p (q j)")
             )
             for h in range(HALVES):
                 cols = slice(h * P, (h + 1) * P)
@@ -115,18 +132,8 @@ def tile_attend_sigm_pgb2q256n512t2048_kernel(tc, qT, k_words, k_scales, vT, vs,
                 nc.scalar.activation(prob[:], score[:].rearrange("p r q -> p q r"), ACT.Sigmoid)
                 probs[b, h] = prob
 
-        v_bf16 = []
-        for b in range(B):
-            v_slots = keep.tile([P, PACK, P], BF16, name="v_slots%d" % b)
-            nc.vector.tensor_copy(dealt(v_slots[:]), v_pool[:].indirect(seq_list(b)))
-            v_turned = psum.tile([P, PACK, DV], BF16, name="v_turned%d" % b)
-            for r in range(PACK):
-                nc.tensor.transpose(v_turned[:, r, :], v_slots[:, r, :], ident_bf16[:])
-            v_b = keep.tile([P, DV, PACK], BF16, name="v_bf16%d" % b, align_bytes=64)
-            nc.scalar.copy(v_b[:], v_turned[:].rearrange("p r e -> p e r"))
-            v_bf16.append(v_b)
-
-        w_bf16 = keep.tile([P, B * HALVES * P * PACK], BF16, name="w_bf16", tag="values_then_weights", align_bytes=64)
+        w_bf16 = keep.tile([P, B * HALVES * P * PACK], BF16, name="w_bf16", align_bytes=64)
+        v_codes = keep.tile([P, B * DV], U32, name="v_codes", tag="queries_then_values1", align_bytes=64)
         units = [(b, h) for b in range(B) for h in range(HALVES)]
         v_mx = {}
 
@@ -138,15 +145,15 @@ def tile_attend_sigm_pgb2q256n512t2048_kernel(tc, qT, k_words, k_scales, vT, vs,
             nc.vector.tensor_tensor(
                 weights(u).rearrange("p (q r) -> p q r", r=PACK),
                 probs[b, h][:],
-                slot_scale[b][:].unsqueeze(1).broadcast_to([P, P, PACK]),
+                slot_scale[b].unsqueeze(1).broadcast_to([P, P, PACK]),
                 MULT,
             )
 
         def quantize_values(b):
-            v_code = keep.tile([P, DV], U32, name="v_code%d" % b, align_bytes=64)
+            v_code = v_codes[:, b * DV : (b + 1) * DV]
             v_scale = keep.tile([P, DV], U8, name="v_scale%d" % b, align_bytes=64)
             nc.vector.quantize_mx(
-                out=v_code[:].bitcast(FP8X4), scales=v_scale[:], in_=v_bf16[b][:].rearrange("p e r -> p (e r)")
+                out=v_code.bitcast(FP8X4), scales=v_scale[:], in_=v_bf16[b][:].rearrange("p e r -> p (e r)")
             )
             v_mx[b] = (v_code, v_scale)
 
@@ -160,7 +167,7 @@ def tile_attend_sigm_pgb2q256n512t2048_kernel(tc, qT, k_words, k_scales, vT, vs,
                 out=y[:],
                 lhsT=w_code[:].bitcast(FP8X4),
                 lhsT_scale=w_scale[:],
-                rhs=v_mx[b][0][:].bitcast(FP8X4),
+                rhs=v_mx[b][0].bitcast(FP8X4),
                 rhs_scale=v_mx[b][1][:],
                 start=True,
                 stop=True,

@@ -15,6 +15,7 @@ U8 = mybir.dt.uint8
 FP8X4 = mybir.dt.float8_e4m3fn_x4
 ACT = mybir.ActivationFunctionType
 MULT = mybir.AluOpType.mult
+ADD = mybir.AluOpType.add
 
 P = 128
 PACK = 4
@@ -30,6 +31,9 @@ def tile_attend_sigm_pgb2q256n512t2048_kernel(tc, qT, k_words, k_scales, vT, vs,
         keep = ctx.enter_context(tc.tile_pool(name="keep", bufs=1))
         psum = ctx.enter_context(tc.psum_pool(name="psum", bufs=1))
 
+        ks_pool = keep.tile([P, T], U8, name="ks_pool")
+        nc.gpsimd.memset(ks_pool[:].bitcast(I32), 0)
+
         offsets = keep.tile([P, B * LIST_COLS], U16, name="offsets")
         nc.sync.dma_start(offsets[:], offs)
 
@@ -42,22 +46,18 @@ def tile_attend_sigm_pgb2q256n512t2048_kernel(tc, qT, k_words, k_scales, vT, vs,
         nc.gpsimd.memset(vs_pool[0:VS_ROW, T // 2 : T], 0.0)
         nc.sync.dma_start(vs_pool[VS_ROW:P, :], vs[0:1, :])
 
-        ks_pool = keep.tile([P, T], U8, name="ks_pool")
-        for quad in range(4):
-            rows = k_scales[0, 4 * quad : 4 * quad + 4, :].bitcast(I32)
-            nc.sync.dma_start(
-                ks_pool[32 * quad : 32 * quad + 32, :].bitcast(I32),
-                rows.unsqueeze(0).broadcast_to([8, 4, T // 4]),
-            )
-
         q_raw = [keep.tile([P, PACK, NQ], F32, name="q_raw", tag="stage%d" % b, align_bytes=64) for b in range(B)]
         kw_pool = keep.tile([P, T], U32, name="kw_pool")
         v_raw = [keep.tile([P, T // 2], F32, name="v_raw%d" % c) for c in range(2)]
-        for c in range(2):
-            nc.sync.dma_start(v_raw[c][:], vT[:, c * (T // 2) : (c + 1) * (T // 2)])
+        nc.sync.dma_start(v_raw[0][:], vT[:, 0 : T // 2])
+        for quad in range(4):
+            nc.sync.dma_start(
+                ks_pool[32 * quad : 32 * quad + 4, :].bitcast(I32), k_scales[0, 4 * quad : 4 * quad + 4, :].bitcast(I32)
+            )
+        nc.sync.dma_start(v_raw[1][:], vT[:, T // 2 : T])
+        nc.sync.dma_start(q_raw[0][:], qT[0].rearrange("(p j) q -> p j q", j=PACK))
         nc.sync.dma_start(kw_pool[:].bitcast(I32), k_words[0].rearrange("p t r -> p (t r)").bitcast(I32))
-        for b in range(B):
-            nc.sync.dma_start(q_raw[b][:], qT[b].rearrange("(p j) q -> p j q", j=PACK))
+        nc.sync.dma_start(q_raw[1][:], qT[1].rearrange("(p j) q -> p j q", j=PACK))
 
         ident_f32 = keep.tile([P, P], F32, name="ident_f32")
         make_identity(nc, ident_f32[:])
@@ -91,29 +91,35 @@ def tile_attend_sigm_pgb2q256n512t2048_kernel(tc, qT, k_words, k_scales, vT, vs,
         v_pool = keep.tile([P, T], BF16, name="v_pool")
         for c in range(2):
             nc.scalar.activation(v_pool[:, c * (T // 2) : (c + 1) * (T // 2)], v_raw[c][:], ACT.Copy)
-        v_bf16 = []
+        v_slots = [keep.tile([P, PACK, P], BF16, name="v_slots%d" % b) for b in range(B)]
         for b in range(B):
-            v_slots = keep.tile([P, PACK, P], BF16, name="v_slots%d" % b)
-            nc.scalar.activation(dealt(v_slots[:]), v_pool[:].indirect(seq_list(b)), ACT.Copy)
-            v_turned = psum.tile([P, PACK, DV], BF16, name="v_turned%d" % b)
+            nc.scalar.activation(dealt(v_slots[b][:]), v_pool[:].indirect(seq_list(b)), ACT.Copy)
+
+        def turn_values(b, bank, v_b):
+            v_turned = psum.tile([P, PACK, DV], BF16, name="v_turned", tag=bank)
             for r in range(PACK):
-                nc.tensor.transpose(v_turned[:, r, :], v_slots[:, r, :], ident_bf16[:])
-            v_b = keep.tile([P, DV, PACK], BF16, name="v_bf16%d" % b, align_bytes=64)
-            nc.scalar.copy(v_b[:], v_turned[:].rearrange("p r e -> p e r"))
-            v_bf16.append(v_b)
+                nc.tensor.transpose(v_turned[:, r, :], v_slots[b][:, r, :], ident_bf16[:])
+            nc.scalar.copy(v_b.rearrange("p (e r) -> p e r", r=PACK), v_turned[:].rearrange("p r e -> p e r"))
+
+        q_bf16 = [
+            keep.tile([P, NQ, PACK], BF16, name="q_bf16", tag="queries_then_values%d" % b, align_bytes=64)
+            for b in range(B)
+        ]
+
+        for b in range(B):
+            nc.gpsimd.tensor_scalar(q_bf16[b][:], q_raw[b][:].rearrange("p j q -> p q j"), 1.0, 0.0, MULT, ADD)
+        v_bf16 = [keep.tile([P, DV * PACK], BF16, name="v_bf16%d" % b, align_bytes=64)[:] for b in range(B)]
+        for b in range(B):
+            turn_values(b, "values%d" % b, v_bf16[b])
 
         probs = {}
         for b in range(B):
-            k_code = keep.tile([P, PACK, P], U32, name="k_code", tag="stage0" if b else "keys0", align_bytes=64)
+            k_code = keep.tile([P, PACK, P], U32, name="k_code%d" % b, align_bytes=64)
             nc.vector.tensor_copy(dealt(k_code[:]), kw_pool[:].indirect(seq_list(b)))
-            q_bf16 = keep.tile([P, NQ, PACK], BF16, name="q_bf16", tag="queries_then_values%d" % b, align_bytes=64)
-            nc.vector.tensor_copy(
-                q_bf16[:].rearrange("p (c i) j -> p c j i", i=4), q_raw[b][:].rearrange("p j (c i) -> p c j i", i=4)
-            )
             q_code = keep.tile([P, NQ], U32, name="q_code%d" % b, align_bytes=64)
             q_scale = keep.tile([P, NQ], U8, name="q_scale%d" % b, align_bytes=64)
             nc.vector.quantize_mx(
-                out=q_code[:].bitcast(FP8X4), scales=q_scale[:], in_=q_bf16[:].rearrange("p q j -> p (q j)")
+                out=q_code[:].bitcast(FP8X4), scales=q_scale[:], in_=q_bf16[b][:].rearrange("p q j -> p (q j)")
             )
             for h in range(HALVES):
                 cols = slice(h * P, (h + 1) * P)
@@ -128,8 +134,8 @@ def tile_attend_sigm_pgb2q256n512t2048_kernel(tc, qT, k_words, k_scales, vT, vs,
                         start=True,
                         stop=True,
                     )
-                prob = keep.tile([P, P, PACK], F32, name="prob%d%d" % (b, h))
-                nc.scalar.activation(prob[:], score[:].rearrange("p r q -> p q r"), ACT.Sigmoid)
+                prob = keep.tile([P, P, PACK], F32, name="prob%d%d" % (b, h))[:]
+                nc.scalar.activation(prob, score[:].rearrange("p r q -> p q r"), ACT.Sigmoid)
                 probs[b, h] = prob
 
         w_bf16 = keep.tile([P, B * HALVES * P * PACK], BF16, name="w_bf16", align_bytes=64)
@@ -144,7 +150,7 @@ def tile_attend_sigm_pgb2q256n512t2048_kernel(tc, qT, k_words, k_scales, vT, vs,
             b, h = units[u]
             nc.vector.tensor_tensor(
                 weights(u).rearrange("p (q r) -> p q r", r=PACK),
-                probs[b, h][:],
+                probs[b, h],
                 slot_scale[b].unsqueeze(1).broadcast_to([P, P, PACK]),
                 MULT,
             )
@@ -153,7 +159,7 @@ def tile_attend_sigm_pgb2q256n512t2048_kernel(tc, qT, k_words, k_scales, vT, vs,
             v_code = v_codes[:, b * DV : (b + 1) * DV]
             v_scale = keep.tile([P, DV], U8, name="v_scale%d" % b, align_bytes=64)
             nc.vector.quantize_mx(
-                out=v_code.bitcast(FP8X4), scales=v_scale[:], in_=v_bf16[b][:].rearrange("p e r -> p (e r)")
+                out=v_code.bitcast(FP8X4), scales=v_scale[:], in_=v_bf16[b]
             )
             v_mx[b] = (v_code, v_scale)
 
@@ -177,9 +183,12 @@ def tile_attend_sigm_pgb2q256n512t2048_kernel(tc, qT, k_words, k_scales, vT, vs,
             nc.sync.dma_start(out[b, h * P : (h + 1) * P, :], result[:])
 
         weigh(0)
-        for u in range(1, len(units)):
-            weigh(u)
-            if units[u - 1][1] == 0:
-                quantize_values(units[u - 1][0])
-            finish(u - 1)
-        finish(len(units) - 1)
+        weigh(1)
+        quantize_values(0)
+        finish(0)
+        weigh(2)
+        finish(1)
+        quantize_values(1)
+        weigh(3)
+        finish(2)
+        finish(3)

@@ -47,7 +47,7 @@ def tile_attend_sigm_pgb2q256n512t2048_kernel(tc, qT, k_words, k_scales, vT, vs,
         nc.sync.dma_start(vs_pool[VS_ROW:P, :], vs[0:1, :])
 
         q_raw = [keep.tile([P, PACK, NQ], F32, name="q_raw", tag="stage%d" % b, align_bytes=64) for b in range(B)]
-        kw_pool = keep.tile([P, T], U32, name="kw_pool")
+        kw_pool = keep.tile([P, T], U32, name="kw_pool", tag="key_pool_then_values", align_bytes=64)
         v_raw = [keep.tile([P, T // 2], F32, name="v_raw%d" % c) for c in range(2)]
         nc.sync.dma_start(v_raw[0][:], vT[:, 0 : T // 2])
         for quad in range(4):
@@ -102,7 +102,7 @@ def tile_attend_sigm_pgb2q256n512t2048_kernel(tc, qT, k_words, k_scales, vT, vs,
             nc.scalar.copy(v_b.rearrange("p (e r) -> p e r", r=PACK), v_turned[:].rearrange("p r e -> p e r"))
 
         q_bf16 = [
-            keep.tile([P, NQ, PACK], BF16, name="q_bf16", tag="queries_then_values%d" % b, align_bytes=64)
+            keep.tile([P, NQ, PACK], BF16, name="q_bf16", tag=["queries0_then_keys", "queries1_then_weights"][b], align_bytes=64)
             for b in range(B)
         ]
 
@@ -114,20 +114,25 @@ def tile_attend_sigm_pgb2q256n512t2048_kernel(tc, qT, k_words, k_scales, vT, vs,
 
         probs = {}
         for b in range(B):
-            k_code = keep.tile([P, PACK, P], U32, name="k_code%d" % b, align_bytes=64)
-            nc.vector.tensor_copy(dealt(k_code[:]), kw_pool[:].indirect(seq_list(b)))
             q_code = keep.tile([P, NQ], U32, name="q_code%d" % b, align_bytes=64)
             q_scale = keep.tile([P, NQ], U8, name="q_scale%d" % b, align_bytes=64)
             nc.vector.quantize_mx(
                 out=q_code[:].bitcast(FP8X4), scales=q_scale[:], in_=q_bf16[b][:].rearrange("p q j -> p (q j)")
             )
+            if b == 0:
+                k_codes = keep.tile([P, B * N], U32, name="k_codes", tag="queries0_then_keys", align_bytes=64)
+                for c in range(B):
+                    nc.vector.tensor_copy(
+                        dealt(k_codes[:, c * N : (c + 1) * N].rearrange("p (r s) -> p r s", r=PACK)),
+                        kw_pool[:].indirect(seq_list(c)),
+                    )
             for h in range(HALVES):
                 cols = slice(h * P, (h + 1) * P)
                 score = psum.tile([P, PACK, P], F32, name="score", tag="bank%d%d" % (b, h))
                 for r in range(PACK):
                     nc.tensor.matmul_mx(
                         out=score[:, r, :],
-                        lhsT=k_code[:, r, :].bitcast(FP8X4),
+                        lhsT=k_codes[:, b * N + r * P : b * N + (r + 1) * P].bitcast(FP8X4),
                         lhsT_scale=k_scale[:, b * N + r * P : b * N + (r + 1) * P],
                         rhs=q_code[:, cols].bitcast(FP8X4),
                         rhs_scale=q_scale[:, cols],
@@ -138,8 +143,8 @@ def tile_attend_sigm_pgb2q256n512t2048_kernel(tc, qT, k_words, k_scales, vT, vs,
                 nc.scalar.activation(prob, score[:].rearrange("p r q -> p q r"), ACT.Sigmoid)
                 probs[b, h] = prob
 
-        w_bf16 = keep.tile([P, B * HALVES * P * PACK], BF16, name="w_bf16", align_bytes=64)
-        v_codes = keep.tile([P, B * DV], U32, name="v_codes", tag="queries_then_values1", align_bytes=64)
+        w_bf16 = keep.tile([P, B * HALVES * P * PACK], BF16, name="w_bf16", tag="queries1_then_weights", align_bytes=64)
+        v_codes = keep.tile([P, B * DV], U32, name="v_codes", tag="key_pool_then_values", align_bytes=64)
         units = [(b, h) for b in range(B) for h in range(HALVES)]
         v_mx = {}
 

@@ -37,10 +37,6 @@ def tile_attend_sigm_pgb2q256n512t2048_kernel(tc, qT, k_words, k_scales, vT, vs,
         offsets = keep.tile([P, B * LIST_COLS], U16, name="offsets")
         nc.sync.dma_start(offsets[:], offs)
 
-        warm = keep.tile([P, 2], F32, name="warm")
-        nc.vector.memset(warm[:, 0:1], 0.0)
-        nc.scalar.activation(warm[:, 1:2], warm[:, 0:1], ACT.Sigmoid)
-
         vs_pool = keep.tile([P, T], F32, name="vs_pool")
         nc.vector.memset(vs_pool[0:VS_ROW, 0 : T // 2], 0.0)
         nc.gpsimd.memset(vs_pool[0:VS_ROW, T // 2 : T], 0.0)

from contextlib import ExitStack

import concourse.mybir as mybir
from concourse.masks import make_identity

B, N, T, D, DV, NQ = 2, 512, 2048, 512, 128, 256
FLOPS = 2 * B * NQ * N * (D + DV)

F32 = mybir.dt.float32
BF16 = mybir.dt.bfloat16
I32 = mybir.dt.int32
U32 = mybir.dt.uint32
U16 = mybir.dt.uint16
U8 = mybir.dt.uint8
FP8X4 = mybir.dt.float8_e4m3fn_x4
ACT = mybir.ActivationFunctionType
MULT = mybir.AluOpType.mult
ADD = mybir.AluOpType.add

P = 128
PACK = 4
RUN = 8
HALVES = NQ // P
LIST_COLS = N // 16
VS_ROW = P - 1


def tile_attend_sigm_pgb2q256n512t2048_kernel(tc, qT, k_words, k_scales, vT, vs, offs, out):
    nc = tc.nc
    with ExitStack() as ctx:
        keep = ctx.enter_context(tc.tile_pool(name="keep", bufs=1))
        psum = ctx.enter_context(tc.psum_pool(name="psum", bufs=1))

        ks_pool = keep.tile([P, T], U8, name="ks_pool")
        nc.gpsimd.memset(ks_pool[:].bitcast(I32), 0)

        offsets = keep.tile([P, B * LIST_COLS], U16, name="offsets")
        nc.sync.dma_start(offsets[:], offs)

        vs_pool = keep.tile([P, T], F32, name="vs_pool")
        nc.vector.memset(vs_pool[0:VS_ROW, 0 : T // 2], 0.0)
        nc.gpsimd.memset(vs_pool[0:VS_ROW, T // 2 : T], 0.0)
        nc.sync.dma_start(vs_pool[VS_ROW:P, :], vs[0:1, :])

        q_raw = [keep.tile([P, PACK, NQ], F32, name="q_raw", tag="stage%d" % b, align_bytes=64) for b in range(B)]
        kw_pool = keep.tile([P, T], U32, name="kw_pool", tag="key_pool_then_values", align_bytes=64)
        v_raw = [keep.tile([P, T // 2], F32, name="v_raw%d" % c) for c in range(2)]
        nc.sync.dma_start(v_raw[0][:], vT[:, 0 : T // 2])
        for quad in range(4):
            nc.sync.dma_start(
                ks_pool[32 * quad : 32 * quad + 4, :].bitcast(I32), k_scales[0, 4 * quad : 4 * quad + 4, :].bitcast(I32)
            )
        nc.sync.dma_start(v_raw[1][:], vT[:, T // 2 : T])
        nc.sync.dma_start(q_raw[0][:], qT[0].rearrange("(p j) q -> p j q", j=PACK))
        nc.sync.dma_start(kw_pool[:].bitcast(I32), k_words[0].rearrange("p t r -> p (t r)").bitcast(I32))
        nc.sync.dma_start(q_raw[1][:], qT[1].rearrange("(p j) q -> p j q", j=PACK))

        ident_f32 = keep.tile([P, P], F32, name="ident_f32")
        make_identity(nc, ident_f32[:])
        ident_bf16 = keep.tile([P, P], BF16, name="ident_bf16")
        make_identity(nc, ident_bf16[:])

        def dealt(ap):
            return ap.rearrange("p r (g i) -> p g r i", i=RUN)

        def seq_list(b):
            return offsets[:, b * LIST_COLS : (b + 1) * LIST_COLS]

        vs_dealt = [keep.tile([P, PACK, P], F32, name="vs_dealt%d" % b) for b in range(B)]
        for b in range(B):
            nc.vector.tensor_copy(dealt(vs_dealt[b][:].bitcast(U32)), vs_pool[:].bitcast(U32).indirect(seq_list(b)))
        ks_slots = keep.tile([P, B * N], U8, name="ks_slots")
        nc.vector.tensor_copy(ks_slots[:], ks_pool[:].indirect(offsets[:]))
        k_scale = keep.tile([P, B * N], U8, name="k_scale", align_bytes=64)
        nc.vector.tensor_copy(
            k_scale[:].bitcast(I32).rearrange("p (b r g w) -> p b r g w", b=B, r=PACK, w=RUN // 4),
            ks_slots[:].bitcast(I32).rearrange("p (b g r w) -> p b r g w", b=B, r=PACK, w=RUN // 4),
        )

        slot_scale = []
        for b in range(B):
            vs_turned = psum.tile([P, PACK, P], F32, name="vs_turned%d" % b)
            for r in range(PACK):
                nc.tensor.transpose(vs_turned[:, r, :], vs_dealt[b][:, r, :], ident_f32[:])
            slot_scale.append(vs_turned[:, :, VS_ROW])

        v_pool = keep.tile([P, T], BF16, name="v_pool")
        for c in range(2):
            nc.scalar.activation(v_pool[:, c * (T // 2) : (c + 1) * (T // 2)], v_raw[c][:], ACT.Copy)
        v_slots = [keep.tile([P, PACK, P], BF16, name="v_slots%d" % b) for b in range(B)]
        for b in range(B):
            nc.scalar.activation(dealt(v_slots[b][:]), v_pool[:].indirect(seq_list(b)), ACT.Copy)

        def turn_values(b, bank, v_b):
            v_turned = psum.tile([P, PACK, DV], BF16, name="v_turned", tag=bank)
            for r in range(PACK):
                nc.tensor.transpose(v_turned[:, r, :], v_slots[b][:, r, :], ident_bf16[:])
            nc.scalar.copy(v_b.rearrange("p (e r) -> p e r", r=PACK), v_turned[:].rearrange("p r e -> p e r"))

        q_bf16 = [
            keep.tile([P, NQ, PACK], BF16, name="q_bf16", tag=["queries0_then_keys", "queries1_then_weights"][b], align_bytes=64)
            for b in range(B)
        ]

        for b in range(B):
            nc.gpsimd.tensor_scalar(q_bf16[b][:], q_raw[b][:].rearrange("p j q -> p q j"), 1.0, 0.0, MULT, ADD)
        v_bf16 = [keep.tile([P, DV * PACK], BF16, name="v_bf16%d" % b, align_bytes=64)[:] for b in range(B)]
        for b in range(B):
            turn_values(b, "values%d" % b, v_bf16[b])

        probs = {}
        for b in range(B):
            q_code = keep.tile([P, NQ], U32, name="q_code%d" % b, align_bytes=64)
            q_scale = keep.tile([P, NQ], U8, name="q_scale%d" % b, align_bytes=64)
            nc.vector.quantize_mx(
                out=q_code[:].bitcast(FP8X4), scales=q_scale[:], in_=q_bf16[b][:].rearrange("p q j -> p (q j)")
            )
            if b == 0:
                k_codes = keep.tile([P, B * N], U32, name="k_codes", tag="queries0_then_keys", align_bytes=64)
                for c in range(B):
                    nc.vector.tensor_copy(
                        dealt(k_codes[:, c * N : (c + 1) * N].rearrange("p (r s) -> p r s", r=PACK)),
                        kw_pool[:].indirect(seq_list(c)),
                    )
            for h in range(HALVES):
                cols = slice(h * P, (h + 1) * P)
                score = psum.tile([P, PACK, P], F32, name="score", tag="bank%d%d" % (b, h))
                for r in range(PACK):
                    nc.tensor.matmul_mx(
                        out=score[:, r, :],
                        lhsT=k_codes[:, b * N + r * P : b * N + (r + 1) * P].bitcast(FP8X4),
                        lhsT_scale=k_scale[:, b * N + r * P : b * N + (r + 1) * P],
                        rhs=q_code[:, cols].bitcast(FP8X4),
                        rhs_scale=q_scale[:, cols],
                        start=True,
                        stop=True,
                    )
                prob = keep.tile([P, P, PACK], F32, name="prob%d%d" % (b, h))[:]
                nc.scalar.activation(prob, score[:].rearrange("p r q -> p q r"), ACT.Sigmoid)
                probs[b, h] = prob

        w_bf16 = keep.tile([P, B * HALVES * P * PACK], BF16, name="w_bf16", tag="queries1_then_weights", align_bytes=64)
        v_codes = keep.tile([P, B * DV], U32, name="v_codes", tag="key_pool_then_values", align_bytes=64)
        units = [(b, h) for b in range(B) for h in range(HALVES)]
        v_mx = {}

        def weights(u):
            return w_bf16[:, u * P * PACK : (u + 1) * P * PACK]

        def weigh(u):
            b, h = units[u]
            nc.vector.tensor_tensor(
                weights(u).rearrange("p (q r) -> p q r", r=PACK),
                probs[b, h],
                slot_scale[b].unsqueeze(1).broadcast_to([P, P, PACK]),
                MULT,
            )

        def quantize_values(b):
            v_code = v_codes[:, b * DV : (b + 1) * DV]
            v_scale = keep.tile([P, DV], U8, name="v_scale%d" % b, align_bytes=64)
            nc.vector.quantize_mx(
                out=v_code.bitcast(FP8X4), scales=v_scale[:], in_=v_bf16[b]
            )
            v_mx[b] = (v_code, v_scale)

        def finish(u):
            b, h = units[u]
            w_code = keep.tile([P, P], U32, name="w_code%d" % u, align_bytes=64)
            w_scale = keep.tile([P, P], U8, name="w_scale%d" % u, align_bytes=64)
            nc.vector.quantize_mx(out=w_code[:].bitcast(FP8X4), scales=w_scale[:], in_=weights(u))
            y = psum.tile([P, DV], F32, name="y", tag="bank%d%d" % (b, h))
            nc.tensor.matmul_mx(
                out=y[:],
                lhsT=w_code[:].bitcast(FP8X4),
                lhsT_scale=w_scale[:],
                rhs=v_mx[b][0].bitcast(FP8X4),
                rhs_scale=v_mx[b][1][:],
                start=True,
                stop=True,
            )
            result = keep.tile([P, DV], F32, name="result%d" % u)
            nc.scalar.activation(result[:], y[:], ACT.Copy, scale=1.0 / 16.0)
            nc.sync.dma_start(out[b, h * P : (h + 1) * P, :], result[:])

        weigh(0)
        weigh(1)
        quantize_values(0)
        finish(0)
        weigh(2)
        finish(1)
        quantize_values(1)
        weigh(3)
        finish(2)
        finish(3)
